import numpy as np
import ml_dtypes


def mxq(x, axis, fmt="e4m3"):
    dtype, down = {"e4m3": (ml_dtypes.float8_e4m3fn, 7), "e5m2": (ml_dtypes.float8_e5m2, 14)}[fmt]
    v = np.moveaxis(np.asarray(x, np.float32).astype(ml_dtypes.bfloat16).astype(np.float64), axis, -1)
    blocks = v.reshape(v.shape[:-1] + (-1, 32))
    amax = np.abs(blocks).max(-1, keepdims=True)
    byte = np.maximum(np.where(amax > 0, np.frexp(amax)[1] - 1 + 127, 0) - down, 1)
    scale = np.exp2(byte - 127.0)
    codes = (blocks / scale).astype(np.float32).astype(dtype).astype(np.float64)
    return np.moveaxis((codes * scale).reshape(v.shape), -1, axis)


WIDE = False


def mx_kscale(k):
    if not WIDE:
        return np.ones(k)
    levels = np.array([10, -10, 5, -5, 0])
    if k % 512:
        return np.exp2(np.random.permutation(np.resize(levels, k // 32))).repeat(32)
    a = np.empty((k // 512, 16))
    for p in range(k // 512):
        a[p, :8] = np.random.permutation(np.resize(levels, 8))
        for g in range(8):
            far = levels[np.abs(levels - a[p, g]) >= 10]
            a[p, g + 8] = far[np.random.randint(len(far))]
    return np.exp2(a.ravel()).repeat(32)


def f64(x):
    return np.asarray(x).astype(np.float64)


def striped(idx):
    return np.tile(idx.reshape(-1, 16).T, (8, 1)).astype(np.uint16)


def unstriped(offs):
    return offs[:16].T.reshape(-1).astype(np.int64)


def pack_weight(w):
    k, n = w.shape
    w = f64(np.asarray(w, np.float32).astype(ml_dtypes.bfloat16)).reshape(k // 32, 32, n)
    amax = np.abs(w).max(1)
    byte = np.clip(np.where(amax > 0, np.frexp(amax)[1] - 1 + 127 - 7, 1), 1, 254)
    scaled = (w * np.exp2(127.0 - byte)[:, None, :]).reshape(k, n).astype(np.float32)
    words = np.ascontiguousarray(scaled.reshape(k // 512, 128, 4, n).transpose(0, 1, 3, 2)).astype(ml_dtypes.float8_e4m3fn).view(np.uint8)
    return words, np.ascontiguousarray(byte.astype(np.uint8).reshape(k // 512, 16, n))


def unpack_weight(words, scales):
    g, p, n, _ = words.shape
    vals = np.ascontiguousarray(words).view(ml_dtypes.float8_e4m3fn).astype(np.float64) * np.repeat(np.exp2(scales.astype(np.float64) - 127.0), 8, axis=1)[..., None]
    return vals.transpose(0, 1, 3, 2).reshape(g * 512, n)


K, T, S, N, H, W = 512, 2048, 512, 512, 512, 2048


def setup_inputs():
    n = np.random.standard_normal
    s = mx_kscale(K)[:, None]
    u = mx_kscale(S)
    packed_xT = pack_weight(n((K, T)) * s)
    return {
        "x_words": packed_xT[0],
        "x_scales": packed_xT[1],
        "wa": (n((K, H)) / np.sqrt(K) / s).astype(np.float32),
        "wb": (n((K, H)) / np.sqrt(K) / s).astype(np.float32),
        "tau": np.random.uniform(0.3, 0.9, (S, 1)).astype(np.float32),
        "gt": (np.random.uniform(0.5, 1.5, (S, 1)) * u[:, None]).astype(np.float32),
        "w1": (n((S, N)) / np.sqrt(S) / u[:, None]).astype(np.float32),
        "tau2": np.random.uniform(0.3, 0.9, (N, 1)).astype(np.float32),
        "offs": striped(np.random.permutation(T)[:S]),
        "two": striped(np.random.permutation(T)[:S]),
        "n1": striped(np.random.permutation(H)),
        "n2": striped(np.random.permutation(H)),
        "n3": striped(np.random.randint(0, H, W)),
    }


def reference(x_words, x_scales, wa, wb, tau, gt, w1, tau2, offs, two, n1, n2, n3):
    x_two = unpack_weight(x_words, x_scales)[:, unstriped(two)]
    d = x_two.T @ mxq(f64(wb), 0, "e4m3")
    top = d.max(axis=1, keepdims=True)
    ea = np.exp(f64(tau) * (d[:, unstriped(n1)] - top))
    xq = unpack_weight(x_words, x_scales)[:, unstriped(offs)]
    y = xq.T @ mxq(f64(wa), 0, "e4m3")
    z = f64(gt) * ((2.0 * ea) * (y - y[:, unstriped(n2)]) - (0.5 * d))
    h = mxq(f64(w1), 0, "e4m3").T @ mxq(z, 0, "e4m3")
    top2 = h.max(axis=1, keepdims=True)
    ea2 = np.exp(f64(tau2) * (h[:, unstriped(n3)] - top2))
    ms = ea2.reshape(N, H, 4).sum(axis=2)
    return np.log(ms + 0.25) - (0.5 * h)

@@ -1,0 +1,204 @@
+from contextlib import ExitStack
+
+import concourse.mybir as mybir
+
+K, T, S, N, H, W = 512, 2048, 512, 512, 512, 2048
+FLOPS = 3 * 2 * 512 * 512 * 512
+
+F32 = mybir.dt.float32
+BF16 = mybir.dt.bfloat16
+I32 = mybir.dt.int32
+U32 = mybir.dt.uint32
+U16 = mybir.dt.uint16
+U8 = mybir.dt.uint8
+FP8X4 = mybir.dt.float8_e4m3fn_x4
+ACT = mybir.ActivationFunctionType
+ALU = mybir.AluOpType
+AX = mybir.AxisListType
+
+P = 128
+PACK = 4
+HALF = 256
+Z_CHUNKS = ((0, 256), (256, 384), (384, 512))
+
+
+def tile_picked_twtpxbegl_none_p_kernel(tc, x_words, x_scales, wa, wb, tau, gt, w1, tau2, offs, two, n1, n2, n3, out):
+    nc = tc.nc
+    with ExitStack() as ctx:
+        keep = ctx.enter_context(tc.tile_pool(name="keep", bufs=1))
+        ring = ctx.enter_context(tc.tile_pool(name="ring", bufs=4))
+        psum = ctx.enter_context(tc.psum_pool(name="psum", bufs=1))
+
+        def held(shape, dtype, name, tag=None):
+            return keep.tile(shape, dtype, name=name, tag=tag or name, align_bytes=64)
+
+        def load_list(src, name):
+            tile = keep.tile(list(src.shape), U16, name=name)
+            nc.sync.dma_start(tile[:], src)
+            return tile
+
+        def load_rows(w, cols, name):
+            raw = held([P, PACK, cols.stop - cols.start], F32, name)
+            nc.sync.dma_start(out=raw[:], in_=w[:, cols].rearrange("(p j) c -> p j c", j=PACK))
+            return raw
+
+        def weave_views(woven, planes):
+            return (woven.rearrange("p (c i) t -> p c t i", i=4), planes.rearrange("p t (c i) -> p c t i", i=4))
+
+        def weave_vector(woven, planes):
+            dst, src = weave_views(woven, planes)
+            nc.vector.tensor_copy(out=dst, in_=src)
+
+        def weave_scalar(woven, planes):
+            dst, src = weave_views(woven, planes)
+            nc.scalar.activation(dst, src, ACT.Copy)
+
+        def quantise(codes, scales, woven):
+            nc.vector.quantize_mx(out=codes.bitcast(FP8X4), scales=scales, in_=woven.rearrange("p c t -> p (c t)"))
+
+        def product(acc, lhs, rhs):
+            nc.tensor.matmul_mx(out=acc, lhsT=lhs[0].bitcast(FP8X4), lhsT_scale=lhs[1], rhs=rhs[0].bitcast(FP8X4), rhs_scale=rhs[1], start=True, stop=True)
+
+        scale_table = held([P, T], U8, "scale_table")
+        nc.gpsimd.memset(scale_table[:].bitcast(I32), 0)
+        offs_t = load_list(offs, "offs_t")
+        word_table = held([P, T], U32, "word_table")
+        nc.sync.dma_start(out=word_table[:].bitcast(I32), in_=x_words[0].rearrange("p n t -> p (n t)").bitcast(I32))
+        two_t = load_list(two, "two_t")
+        for q in range(4):
+            nc.scalar.dma_start(out=scale_table[32 * q : 32 * q + 4, :].bitcast(I32), in_=x_scales[0, 4 * q : 4 * q + 4, :].bitcast(I32))
+        halves = [slice(0, HALF), slice(HALF, 2 * HALF)]
+        wa_raw = [load_rows(wa, cols, "wa_raw%d" % h) for h, cols in enumerate(halves)]
+        gt_t = held([P, PACK], F32, "gt_t")
+        nc.sync.dma_start(out=gt_t[:], in_=gt.rearrange("(p t) o -> p (t o)", t=PACK))
+        n2_t = load_list(n2, "n2_t")
+        wb_raw = [load_rows(wb, cols, "wb_raw%d" % h) for h, cols in enumerate(halves)]
+        tau_t = held([P, PACK], F32, "tau_t")
+        nc.sync.dma_start(out=tau_t[:], in_=tau.rearrange("(p t) o -> p (t o)", t=PACK))
+        n1_t = load_list(n1, "n1_t")
+        w1_raw = load_rows(w1, slice(0, N), "w1_raw")
+        n3_t = load_list(n3, "n3_t")
+        tau2_t = held([P, PACK], F32, "tau2_t")
+        with nc.allow_non_contiguous_dma(reason="one rate a partition"):
+            nc.sync.dma_start(out=tau2_t[:], in_=tau2.rearrange("(b p) o -> p (b o)", p=P))
+
+        def pick(table, lst, dtype, name):
+            picked = held([P, S], dtype, name + "_picked", tag="picked")
+            dealt = held([P, S], dtype, name)
+            nc.vector.tensor_copy(picked[:], table[:].indirect(lst[:]))
+            nc.vector.tensor_copy(out=dealt[:].rearrange("p (t m) -> p t m", t=PACK), in_=picked[:].rearrange("p (m t) -> p t m", t=PACK))
+            return dealt
+
+
+        xy_scales = pick(scale_table, offs_t, U8, "xy_scales")
+        xd_scales = pick(scale_table, two_t, U8, "xd_scales")
+        xy = (pick(word_table, offs_t, U32, "xy_words"), xy_scales)
+        wa_q = (held([P, H], U32, "wa_codes"), held([P, H], U8, "wa_scales"))
+        for h, cols in enumerate(halves):
+            woven = held([P, HALF, PACK], BF16, "wa_woven%d" % h, tag="woven" if h else None)
+            weave_scalar(woven[:], wa_raw[h][:])
+            quantise(wa_q[0][:, cols], wa_q[1][:, cols], woven[:])
+
+        gt_twice = held([P, PACK], F32, "gt_twice")
+        gt_neg_half = held([P, PACK], F32, "gt_neg_half")
+        nc.gpsimd.tensor_scalar(gt_twice[:], gt_t[:], 2.0, 0.0, ALU.mult, ALU.add)
+        nc.gpsimd.tensor_scalar(gt_neg_half[:], gt_t[:], -0.5, 0.0, ALU.mult, ALU.add)
+        tau_neg = held([P, PACK], F32, "tau_neg")
+        tau2_neg = held([P, PACK], F32, "tau2_neg")
+        nc.gpsimd.tensor_scalar(tau_neg[:], tau_t[:], -1.0, 0.0, ALU.mult, ALU.add)
+        nc.gpsimd.tensor_scalar(tau2_neg[:], tau2_t[:], -1.0, 0.0, ALU.mult, ALU.add)
+        quarter = held([P, 1], F32, "quarter")
+        nc.gpsimd.memset(quarter[:], 0.25)
+
+        def rows(pair, t):
+            return (pair[0][:, t * P : (t + 1) * P], pair[1][:, t * P : (t + 1) * P])
+
+        h_win = [held([P, 2 * H], F32, "h_win%d" % t) for t in range(PACK)]
+        y_win = []
+        for t in range(PACK):
+            bank = psum.tile([P, H], F32, name="y%d" % t, tag="bank%d" % t)
+            product(bank[:], rows(xy, t), (wa_q[0][:], wa_q[1][:]))
+            win = held([P, H], F32, "y_win%d" % t)
+            nc.scalar.activation(win[:], bank[:], ACT.Copy, scale=gt_twice[:, t : t + 1])
+            for h in range(2):
+                nc.scalar.activation(h_win[t][:, H + h * HALF : H + (h + 1) * HALF], win[:].indirect(n2_t[:, 16 * h : 16 * (h + 1)]), ACT.Copy)
+            y_win.append(win)
+
+        xd = (pick(word_table, two_t, U32, "xd_words"), xd_scales)
+        wb_q = (held([P, H], U32, "wb_codes"), held([P, H], U8, "wb_scales"))
+        woven = held([P, H, PACK], BF16, "wb_woven", tag="woven")
+        for h, cols in enumerate(halves):
+            weave_vector(woven[:, cols, :], wb_raw[h][:])
+        quantise(wb_q[0][:], wb_q[1][:], woven[:])
+        d_bank, d_win = [], []
+        top = held([P, PACK], F32, "top")
+        bias = held([P, PACK], F32, "bias")
+        for t in range(PACK):
+            bank = psum.tile([P, H], F32, name="d%d" % t, tag="bank%d" % (PACK + t))
+            product(bank[:], rows(xd, t), (wb_q[0][:], wb_q[1][:]))
+            win = held([P, H], F32, "d_win%d" % t)
+            nc.vector.tensor_scalar(win[:], bank[:], 1.0, None, ALU.mult, ALU.max, accum_out=top[:, t : t + 1])
+            nc.gpsimd.tensor_tensor(bias[:, t : t + 1], top[:, t : t + 1], tau_neg[:, t : t + 1], ALU.mult)
+            d_bank.append(bank)
+            d_win.append(win)
+
+        y_diff = held([P, PACK, H], F32, "y_diff")
+        for t in range(PACK):
+            nc.vector.tensor_tensor(y_diff[:, t, :], y_win[t][:], h_win[t][:, H:], ALU.subtract)
+
+        w1_codes = held([P, N], U32, "w1_codes")
+        w1_scales = held([P, N], U8, "w1_scales")
+
+        def quantise_w1(b):
+            cols = slice(b * P, (b + 1) * P)
+            woven = held([P, P, PACK], BF16, "w1_woven%d" % b, tag="top2_part" if b else "woven")
+            weave_vector(woven[:], w1_raw[:, :, cols])
+            quantise(w1_codes[:, cols], w1_scales[:, cols], woven[:])
+
+        quantise_w1(0)
+
+        h_bank = [psum.tile([P, H], F32, name="h%d" % b, tag="bank%d" % b) for b in range(PACK)]
+        z_codes = held([P, H], U32, "z_codes")
+        z_scales = held([P, H], U8, "z_scales")
+        top2_part = held([P, len(Z_CHUNKS)], F32, "top2_part")
+        for c, (lo, hi) in enumerate(Z_CHUNKS):
+            width = hi - lo
+            z_planes = held([P, PACK, width], BF16, "z_planes%d" % c)
+            ea = held([P, PACK, width], F32, "ea%d" % c)
+            mixed = held([P, PACK, width], F32, "mixed%d" % c)
+            for t in range(PACK):
+                nc.scalar.activation(ea[:, t, :], d_win[t][:].indirect(n1_t[:, lo // 16 : hi // 16]), ACT.Exp, bias=bias[:, t : t + 1], scale=tau_t[:, t : t + 1])
+            for pair in (slice(0, 2), slice(2, 4)):
+                nc.vector.tensor_tensor(mixed[:, pair, :], ea[:, pair, :], y_diff[:, pair, lo:hi], ALU.mult)
+                for t in range(pair.start, pair.stop):
+                    nc.vector.scalar_tensor_tensor(z_planes[:, t, :], d_bank[t][:, lo:hi], gt_neg_half[:, t : t + 1], mixed[:, t, :], ALU.mult, ALU.add)
+            woven = held([P, width, PACK], BF16, "z_woven%d" % c)
+            weave_vector(woven[:], z_planes[:])
+            quantise(z_codes[:, lo:hi], z_scales[:, lo:hi], woven[:])
+            product(h_bank[0][:, lo:hi], rows((w1_codes, w1_scales), 0), (z_codes[:, lo:hi], z_scales[:, lo:hi]))
+            nc.vector.tensor_scalar(h_win[0][:, lo:hi], h_bank[0][:, lo:hi], 1.0, None, ALU.mult, ALU.max, accum_out=top2_part[:, c : c + 1])
+
+        top2 = held([P, PACK], F32, "top2")
+        bias2 = held([P, PACK], F32, "bias2")
+        sums = held([P, PACK, H], F32, "sums")
+        for b in range(PACK):
+            if b == 0:
+                nc.vector.tensor_reduce(top2[:, 0:1], top2_part[:], AX.X, ALU.max)
+            else:
+                quantise_w1(b)
+                product(h_bank[b][:], rows((w1_codes, w1_scales), b), (z_codes[:], z_scales[:]))
+                nc.vector.tensor_scalar(h_win[b][:, :H], h_bank[b][:], 1.0, None, ALU.mult, ALU.max, accum_out=top2[:, b : b + 1])
+            nc.vector.tensor_tensor(bias2[:, b : b + 1], top2[:, b : b + 1], tau2_neg[:, b : b + 1], ALU.mult)
+        for b in range(PACK):
+            for c in range(PACK):
+                ea2 = ring.tile([P, H], F32, name="ea2")
+                nc.scalar.activation(ea2[:], h_win[b][:].indirect(n3_t[:, 32 * c : 32 * (c + 1)]), ACT.Exp, bias=bias2[:, b : b + 1], scale=tau2_t[:, b : b + 1])
+                nc.vector.tensor_reduce(sums[:, b, c * P : (c + 1) * P], ea2[:].rearrange("p (j t) -> p j t", t=PACK), AX.X, ALU.add)
+
+        logs = held([P, PACK, H], F32, "logs", tag="h_win%d" % (PACK - 1))
+        pieces = [(0, 0, H), (1, 0, H), (2, 0, H), (3, 0, HALF), (3, HALF, H)]
+        for b, lo, hi in pieces:
+            nc.scalar.activation(logs[:, b, lo:hi], sums[:, b, lo:hi], ACT.Ln, bias=quarter[:])
+            result = held([P, hi - lo], F32, "result%d_%d" % (b, lo))
+            nc.vector.scalar_tensor_tensor(result[:], h_bank[b][:, lo:hi], -0.5, logs[:, b, lo:hi], ALU.mult, ALU.add)
+            nc.sync.dma_start(out=out[b * P : (b + 1) * P, lo:hi], in_=result[:])

@@ -19,18 +19,22 @@ AX = mybir.AxisListType
 P = 128
 PACK = 4
 HALF = 256
-Z_CHUNKS = ((0, 256), (256, 384), (384, 512))
+Z_CHUNKS = ((0, 256), (256, 512))
 
 
 def tile_picked_twtpxbegl_none_p_kernel(tc, x_words, x_scales, wa, wb, tau, gt, w1, tau2, offs, two, n1, n2, n3, out):
     nc = tc.nc
     with ExitStack() as ctx:
         keep = ctx.enter_context(tc.tile_pool(name="keep", bufs=1))
-        ring = ctx.enter_context(tc.tile_pool(name="ring", bufs=4))
+        ring = ctx.enter_context(tc.tile_pool(name="ring", bufs=8))
+        stage = ctx.enter_context(tc.tile_pool(name="stage", bufs=1))
         psum = ctx.enter_context(tc.psum_pool(name="psum", bufs=1))
 
         def held(shape, dtype, name, tag=None):
             return keep.tile(shape, dtype, name=name, tag=tag or name, align_bytes=64)
+
+        def staged(shape, dtype, name, offset):
+            return stage.tile(shape, dtype, name=name, align_bytes=64, offset=offset)
 
         def load_list(src, name):
             tile = keep.tile(list(src.shape), U16, name=name)
@@ -62,17 +66,17 @@ def tile_picked_twtpxbegl_none_p_kernel(tc, x_words, x_scales, wa, wb, tau, gt, 
         scale_table = held([P, T], U8, "scale_table")
         nc.gpsimd.memset(scale_table[:].bitcast(I32), 0)
         offs_t = load_list(offs, "offs_t")
-        word_table = held([P, T], U32, "word_table")
-        nc.sync.dma_start(out=word_table[:].bitcast(I32), in_=x_words[0].rearrange("p n t -> p (n t)").bitcast(I32))
-        two_t = load_list(two, "two_t")
         for q in range(4):
             nc.scalar.dma_start(out=scale_table[32 * q : 32 * q + 4, :].bitcast(I32), in_=x_scales[0, 4 * q : 4 * q + 4, :].bitcast(I32))
         halves = [slice(0, HALF), slice(HALF, 2 * HALF)]
         wa_raw = [load_rows(wa, cols, "wa_raw%d" % h) for h, cols in enumerate(halves)]
+        two_t = load_list(two, "two_t")
+        word_table = held([P, T], U32, "word_table")
+        nc.sync.dma_start(out=word_table[:].bitcast(I32), in_=x_words[0].rearrange("p n t -> p (n t)").bitcast(I32))
         gt_t = held([P, PACK], F32, "gt_t")
         nc.sync.dma_start(out=gt_t[:], in_=gt.rearrange("(p t) o -> p (t o)", t=PACK))
-        n2_t = load_list(n2, "n2_t")
         wb_raw = [load_rows(wb, cols, "wb_raw%d" % h) for h, cols in enumerate(halves)]
+        n2_t = load_list(n2, "n2_t")
         tau_t = held([P, PACK], F32, "tau_t")
         nc.sync.dma_start(out=tau_t[:], in_=tau.rearrange("(p t) o -> p (t o)", t=PACK))
         n1_t = load_list(n1, "n1_t")
@@ -82,31 +86,36 @@ def tile_picked_twtpxbegl_none_p_kernel(tc, x_words, x_scales, wa, wb, tau, gt, 
         with nc.allow_non_contiguous_dma(reason="one rate a partition"):
             nc.sync.dma_start(out=tau2_t[:], in_=tau2.rearrange("(b p) o -> p (b o)", p=P))
 
-        def pick(table, lst, dtype, name):
-            picked = held([P, S], dtype, name + "_picked", tag="picked")
-            dealt = held([P, S], dtype, name)
+        def pick(table, lst, picked):
             nc.vector.tensor_copy(picked[:], table[:].indirect(lst[:]))
+            return picked
+
+        def deal(picked, dtype, name, tag=None):
+            dealt = held([P, S], dtype, name, tag=tag)
             nc.vector.tensor_copy(out=dealt[:].rearrange("p (t m) -> p t m", t=PACK), in_=picked[:].rearrange("p (m t) -> p t m", t=PACK))
             return dealt
 
 
-        xy_scales = pick(scale_table, offs_t, U8, "xy_scales")
-        xd_scales = pick(scale_table, two_t, U8, "xd_scales")
-        xy = (pick(word_table, offs_t, U32, "xy_words"), xy_scales)
+        xy_scales = deal(pick(scale_table, offs_t, held([P, S], U8, "xy_scales_picked")), U8, "xy_scales")
         wa_q = (held([P, H], U32, "wa_codes"), held([P, H], U8, "wa_scales"))
         for h, cols in enumerate(halves):
-            woven = held([P, HALF, PACK], BF16, "wa_woven%d" % h, tag="woven" if h else None)
+            woven = held([P, HALF, PACK], BF16, "wa_woven%d" % h, tag=None)
             weave_scalar(woven[:], wa_raw[h][:])
             quantise(wa_q[0][:, cols], wa_q[1][:, cols], woven[:])
-
-        gt_twice = held([P, PACK], F32, "gt_twice")
         gt_neg_half = held([P, PACK], F32, "gt_neg_half")
-        nc.gpsimd.tensor_scalar(gt_twice[:], gt_t[:], 2.0, 0.0, ALU.mult, ALU.add)
-        nc.gpsimd.tensor_scalar(gt_neg_half[:], gt_t[:], -0.5, 0.0, ALU.mult, ALU.add)
-        tau_neg = held([P, PACK], F32, "tau_neg")
-        tau2_neg = held([P, PACK], F32, "tau2_neg")
-        nc.gpsimd.tensor_scalar(tau_neg[:], tau_t[:], -1.0, 0.0, ALU.mult, ALU.add)
-        nc.gpsimd.tensor_scalar(tau2_neg[:], tau2_t[:], -1.0, 0.0, ALU.mult, ALU.add)
+        nc.scalar.activation(gt_neg_half[:], gt_t[:], ACT.Copy, scale=-0.5)
+        xy = (deal(pick(word_table, offs_t, staged([P, S], U32, "xy_words_picked", 0)), U32, "xy_words"), xy_scales)
+        xd_words_picked = pick(word_table, two_t, staged([P, S], U32, "xd_words_picked", 1024))
+        xd_scales_picked = pick(scale_table, two_t, staged([P, S], U8, "xd_scales_picked", 0))
+        xd = (deal(xd_words_picked, U32, "xd_words"), deal(xd_scales_picked, U8, "xd_scales"))
+        wb_q = (held([P, H], U32, "wb_codes"), held([P, H], U8, "wb_scales"))
+        for h, cols in enumerate(halves):
+            woven = staged([P, HALF, PACK], BF16, "wb_woven1", 1024) if h else held([P, HALF, PACK], BF16, "wb_woven0")
+            (weave_vector if h else weave_scalar)(woven[:], wb_raw[h][:])
+            quantise(wb_q[0][:, cols], wb_q[1][:, cols], woven[:])
+
+        gt_twice = held([P, PACK], F32, "gt_twice", tag="wb_raw0")
+        nc.scalar.activation(gt_twice[:], gt_t[:], ACT.Copy, scale=2.0)
         quarter = held([P, 1], F32, "quarter")
         nc.gpsimd.memset(quarter[:], 0.25)
 
@@ -114,7 +123,7 @@ def tile_picked_twtpxbegl_none_p_kernel(tc, x_words, x_scales, wa, wb, tau, gt, 
             return (pair[0][:, t * P : (t + 1) * P], pair[1][:, t * P : (t + 1) * P])
 
         h_win = [held([P, 2 * H], F32, "h_win%d" % t) for t in range(PACK)]
-        y_win = []
+        y_diff = held([P, PACK, H], F32, "y_diff")
         for t in range(PACK):
             bank = psum.tile([P, H], F32, name="y%d" % t, tag="bank%d" % t)
             product(bank[:], rows(xy, t), (wa_q[0][:], wa_q[1][:]))
@@ -122,14 +131,8 @@ def tile_picked_twtpxbegl_none_p_kernel(tc, x_words, x_scales, wa, wb, tau, gt, 
             nc.scalar.activation(win[:], bank[:], ACT.Copy, scale=gt_twice[:, t : t + 1])
             for h in range(2):
                 nc.scalar.activation(h_win[t][:, H + h * HALF : H + (h + 1) * HALF], win[:].indirect(n2_t[:, 16 * h : 16 * (h + 1)]), ACT.Copy)
-            y_win.append(win)
+            nc.gpsimd.tensor_tensor(y_diff[:, t, :], win[:], h_win[t][:, H:], ALU.subtract)
 
-        xd = (pick(word_table, two_t, U32, "xd_words"), xd_scales)
-        wb_q = (held([P, H], U32, "wb_codes"), held([P, H], U8, "wb_scales"))
-        woven = held([P, H, PACK], BF16, "wb_woven", tag="woven")
-        for h, cols in enumerate(halves):
-            weave_vector(woven[:, cols, :], wb_raw[h][:])
-        quantise(wb_q[0][:], wb_q[1][:], woven[:])
         d_bank, d_win = [], []
         top = held([P, PACK], F32, "top")
         bias = held([P, PACK], F32, "bias")
@@ -138,60 +141,87 @@ def tile_picked_twtpxbegl_none_p_kernel(tc, x_words, x_scales, wa, wb, tau, gt, 
             product(bank[:], rows(xd, t), (wb_q[0][:], wb_q[1][:]))
             win = held([P, H], F32, "d_win%d" % t)
             nc.vector.tensor_scalar(win[:], bank[:], 1.0, None, ALU.mult, ALU.max, accum_out=top[:, t : t + 1])
-            nc.gpsimd.tensor_tensor(bias[:, t : t + 1], top[:, t : t + 1], tau_neg[:, t : t + 1], ALU.mult)
             d_bank.append(bank)
             d_win.append(win)
-
-        y_diff = held([P, PACK, H], F32, "y_diff")
-        for t in range(PACK):
-            nc.vector.tensor_tensor(y_diff[:, t, :], y_win[t][:], h_win[t][:, H:], ALU.subtract)
+            if t % 2:
+                pair = slice(t - 1, t + 1)
+                nc.vector.scalar_tensor_tensor(bias[:, pair], top[:, pair], -1.0, tau_t[:, pair], ALU.mult, ALU.mult)
 
         w1_codes = held([P, N], U32, "w1_codes")
         w1_scales = held([P, N], U8, "w1_scales")
 
         def quantise_w1(b):
             cols = slice(b * P, (b + 1) * P)
-            woven = held([P, P, PACK], BF16, "w1_woven%d" % b, tag="top2_part" if b else "woven")
+            woven = held([P, P, PACK], BF16, "w1_woven%d" % b, tag="top2_0") if b else staged([P, P, PACK], BF16, "w1_woven0", 1024)
             weave_vector(woven[:], w1_raw[:, :, cols])
             quantise(w1_codes[:, cols], w1_scales[:, cols], woven[:])
 
         quantise_w1(0)
 
-        h_bank = [psum.tile([P, H], F32, name="h%d" % b, tag="bank%d" % b) for b in range(PACK)]
-        z_codes = held([P, H], U32, "z_codes")
-        z_scales = held([P, H], U8, "z_scales")
-        top2_part = held([P, len(Z_CHUNKS)], F32, "top2_part")
-        for c, (lo, hi) in enumerate(Z_CHUNKS):
+        top2_part = held([P, 1], F32, "top2_part")
+        z_rows, z_woven, z_q = {}, {}, {}
+
+        def make_z(c):
+            lo, hi = Z_CHUNKS[c]
             width = hi - lo
             z_planes = held([P, PACK, width], BF16, "z_planes%d" % c)
             ea = held([P, PACK, width], F32, "ea%d" % c)
-            mixed = held([P, PACK, width], F32, "mixed%d" % c)
+            mixed = held([P, PACK, width], F32, "mixed%d" % c, tag="mixed")
+            group = 2
             for t in range(PACK):
                 nc.scalar.activation(ea[:, t, :], d_win[t][:].indirect(n1_t[:, lo // 16 : hi // 16]), ACT.Exp, bias=bias[:, t : t + 1], scale=tau_t[:, t : t + 1])
-            for pair in (slice(0, 2), slice(2, 4)):
-                nc.vector.tensor_tensor(mixed[:, pair, :], ea[:, pair, :], y_diff[:, pair, lo:hi], ALU.mult)
-                for t in range(pair.start, pair.stop):
+            for first in range(0, PACK, group):
+                ts = slice(first, first + group)
+                nc.vector.tensor_tensor(mixed[:, ts, :], ea[:, ts, :], y_diff[:, ts, lo:hi], ALU.mult)
+                for t in range(ts.start, ts.stop):
                     nc.vector.scalar_tensor_tensor(z_planes[:, t, :], d_bank[t][:, lo:hi], gt_neg_half[:, t : t + 1], mixed[:, t, :], ALU.mult, ALU.add)
-            woven = held([P, width, PACK], BF16, "z_woven%d" % c)
-            weave_vector(woven[:], z_planes[:])
-            quantise(z_codes[:, lo:hi], z_scales[:, lo:hi], woven[:])
-            product(h_bank[0][:, lo:hi], rows((w1_codes, w1_scales), 0), (z_codes[:, lo:hi], z_scales[:, lo:hi]))
-            nc.vector.tensor_scalar(h_win[0][:, lo:hi], h_bank[0][:, lo:hi], 1.0, None, ALU.mult, ALU.max, accum_out=top2_part[:, c : c + 1])
+            z_rows[c] = z_planes
 
-        top2 = held([P, PACK], F32, "top2")
+        def weave_z(c, weave):
+            lo, hi = Z_CHUNKS[c]
+            z_woven[c] = held([P, hi - lo, PACK], BF16, "z_woven%d" % c)
+            weave(z_woven[c][:], z_rows[c][:])
+
+        def quantise_z(c, tag=None):
+            lo, hi = Z_CHUNKS[c]
+            z_q[c] = (held([P, hi - lo], U32, "z_codes%d" % c, tag=tag), held([P, hi - lo], U8, "z_scales%d" % c))
+            quantise(z_q[c][0][:], z_q[c][1][:], z_woven[c][:])
+
+        def h_product(bank, b, c):
+            lo, hi = Z_CHUNKS[c]
+            product(bank[:, lo:hi], rows((w1_codes, w1_scales), b), (z_q[c][0][:], z_q[c][1][:]))
+
+        def first_rows(c, start, top_so_far):
+            lo, hi = Z_CHUNKS[c]
+            bank = psum.tile([P, H], F32, name="h0_%d" % c, tag="bank%d" % c)
+            h_product(bank, 0, c)
+            nc.vector.tensor_scalar(h_win[0][:, lo:hi], bank[:, lo:hi], 1.0, start, ALU.mult, ALU.max, accum_out=top_so_far)
+
+        top2 = [held([P, 1], F32, "top2_%d" % b) for b in range(PACK)]
+        make_z(0)
+        make_z(1)
+        weave_z(0, weave_scalar)
+        weave_z(1, weave_vector)
+        quantise_z(0, tag="ea1")
+        first_rows(0, None, top2_part[:])
+        quantise_z(1)
+        first_rows(1, top2_part[:], top2[0][:])
+
         bias2 = held([P, PACK], F32, "bias2")
+        h_rows = [h_win[0]]
         sums = held([P, PACK, H], F32, "sums")
         for b in range(PACK):
-            if b == 0:
-                nc.vector.tensor_reduce(top2[:, 0:1], top2_part[:], AX.X, ALU.max)
-            else:
+            if b:
                 quantise_w1(b)
-                product(h_bank[b][:], rows((w1_codes, w1_scales), b), (z_codes[:], z_scales[:]))
-                nc.vector.tensor_scalar(h_win[b][:, :H], h_bank[b][:], 1.0, None, ALU.mult, ALU.max, accum_out=top2[:, b : b + 1])
-            nc.vector.tensor_tensor(bias2[:, b : b + 1], top2[:, b : b + 1], tau2_neg[:, b : b + 1], ALU.mult)
+                bank = psum.tile([P, H], F32, name="h%d" % b, tag="bank%d" % b)
+                for c in range(len(Z_CHUNKS)):
+                    h_product(bank, b, c)
+                h_rows.append(bank)
+                nc.vector.tensor_scalar(h_win[b][:, :H], bank[:], 1.0, None, ALU.mult, ALU.max, accum_out=top2[b][:])
+            nc.vector.scalar_tensor_tensor(bias2[:, b : b + 1], top2[b][:], -1.0, tau2_t[:, b : b + 1], ALU.mult, ALU.mult)
         for b in range(PACK):
             for c in range(PACK):
-                ea2 = ring.tile([P, H], F32, name="ea2")
+                ea2 = ring.tile([P, H], F32, name="members")
                 nc.scalar.activation(ea2[:], h_win[b][:].indirect(n3_t[:, 32 * c : 32 * (c + 1)]), ACT.Exp, bias=bias2[:, b : b + 1], scale=tau2_t[:, b : b + 1])
                 nc.vector.tensor_reduce(sums[:, b, c * P : (c + 1) * P], ea2[:].rearrange("p (j t) -> p j t", t=PACK), AX.X, ALU.add)
 
@@ -200,5 +230,5 @@ def tile_picked_twtpxbegl_none_p_kernel(tc, x_words, x_scales, wa, wb, tau, gt, 
         for b, lo, hi in pieces:
             nc.scalar.activation(logs[:, b, lo:hi], sums[:, b, lo:hi], ACT.Ln, bias=quarter[:])
             result = held([P, hi - lo], F32, "result%d_%d" % (b, lo))
-            nc.vector.scalar_tensor_tensor(result[:], h_bank[b][:, lo:hi], -0.5, logs[:, b, lo:hi], ALU.mult, ALU.add)
+            nc.vector.scalar_tensor_tensor(result[:], h_rows[b][:, lo:hi], -0.5, logs[:, b, lo:hi], ALU.mult, ALU.add)
             nc.sync.dma_start(out=out[b * P : (b + 1) * P, lo:hi], in_=result[:])

@@ -26,7 +26,7 @@ def tile_picked_twtpxbegl_none_p_kernel(tc, x_words, x_scales, wa, wb, tau, gt, 
     nc = tc.nc
     with ExitStack() as ctx:
         keep = ctx.enter_context(tc.tile_pool(name="keep", bufs=1))
-        ring = ctx.enter_context(tc.tile_pool(name="ring", bufs=8))
+        ring = ctx.enter_context(tc.tile_pool(name="ring", bufs=3))
         stage = ctx.enter_context(tc.tile_pool(name="stage", bufs=1))
         psum = ctx.enter_context(tc.psum_pool(name="psum", bufs=1))
 
@@ -46,15 +46,15 @@ def tile_picked_twtpxbegl_none_p_kernel(tc, x_words, x_scales, wa, wb, tau, gt, 
             nc.sync.dma_start(out=raw[:], in_=w[:, cols].rearrange("(p j) c -> p j c", j=PACK))
             return raw
 
-        def weave_views(woven, planes):
-            return (woven.rearrange("p (c i) t -> p c t i", i=4), planes.rearrange("p t (c i) -> p c t i", i=4))
+        def weave_views(woven, planes, run):
+            return (woven.rearrange("p (c i) t -> p c t i", i=run), planes.rearrange("p t (c i) -> p c t i", i=run))
 
-        def weave_vector(woven, planes):
-            dst, src = weave_views(woven, planes)
+        def weave_vector(woven, planes, run=4):
+            dst, src = weave_views(woven, planes, run)
             nc.vector.tensor_copy(out=dst, in_=src)
 
-        def weave_scalar(woven, planes):
-            dst, src = weave_views(woven, planes)
+        def weave_scalar(woven, planes, run=4):
+            dst, src = weave_views(woven, planes, run)
             nc.scalar.activation(dst, src, ACT.Copy)
 
         def quantise(codes, scales, woven):
@@ -92,7 +92,8 @@ def tile_picked_twtpxbegl_none_p_kernel(tc, x_words, x_scales, wa, wb, tau, gt, 
 
         def deal(picked, dtype, name, tag=None):
             dealt = held([P, S], dtype, name, tag=tag)
-            nc.vector.tensor_copy(out=dealt[:].rearrange("p (t m) -> p t m", t=PACK), in_=picked[:].rearrange("p (m t) -> p t m", t=PACK))
+            run = 4 if dtype == U32 else 16
+            nc.vector.tensor_copy(out=dealt[:].rearrange("p (t c i) -> p c t i", t=PACK, i=run), in_=picked[:].rearrange("p (c i t) -> p c t i", t=PACK, i=run))
             return dealt
 
 
@@ -122,30 +123,34 @@ def tile_picked_twtpxbegl_none_p_kernel(tc, x_words, x_scales, wa, wb, tau, gt, 
         def rows(pair, t):
             return (pair[0][:, t * P : (t + 1) * P], pair[1][:, t * P : (t + 1) * P])
 
-        h_win = [held([P, 2 * H], F32, "h_win%d" % t) for t in range(PACK)]
-        y_diff = held([P, PACK, H], F32, "y_diff")
+        h_win = [held([P, 2 * W], F32, "h_win%d" % t) for t in range(PACK)]
+        y_diff = held([P, PACK - 1, H], F32, "y_diff")
         for t in range(PACK):
             bank = psum.tile([P, H], F32, name="y%d" % t, tag="bank%d" % t)
             product(bank[:], rows(xy, t), (wa_q[0][:], wa_q[1][:]))
-            win = held([P, H], F32, "y_win%d" % t)
-            nc.scalar.activation(win[:], bank[:], ACT.Copy, scale=gt_twice[:, t : t + 1])
-            for h in range(2):
-                nc.scalar.activation(h_win[t][:, H + h * HALF : H + (h + 1) * HALF], win[:].indirect(n2_t[:, 16 * h : 16 * (h + 1)]), ACT.Copy)
-            nc.gpsimd.tensor_tensor(y_diff[:, t, :], win[:], h_win[t][:, H:], ALU.subtract)
+            win = held([P, H + 16], F32, "y_win%d" % t)
+            nc.scalar.activation(win[:, :H], bank[:], ACT.Copy, scale=gt_twice[:, t : t + 1])
+            fetched = held([P, H], F32, "y_fetched%d" % t)
+            nc.scalar.activation(fetched[:], win[:].indirect(n2_t[:]), ACT.Copy)
+            if t < PACK - 1:
+                nc.gpsimd.tensor_tensor(y_diff[:, t, :], win[:, :H], fetched[:], ALU.subtract)
+        y_last, fetched_last = win, fetched
 
         d_bank, d_win = [], []
-        top = held([P, PACK], F32, "top")
+        top = [held([P, 2], F32, "top%d" % pair) for pair in range(2)]
         bias = held([P, PACK], F32, "bias")
         for t in range(PACK):
             bank = psum.tile([P, H], F32, name="d%d" % t, tag="bank%d" % (PACK + t))
             product(bank[:], rows(xd, t), (wb_q[0][:], wb_q[1][:]))
             win = held([P, H], F32, "d_win%d" % t)
-            nc.vector.tensor_scalar(win[:], bank[:], 1.0, None, ALU.mult, ALU.max, accum_out=top[:, t : t + 1])
+            nc.vector.tensor_scalar(win[:], bank[:], 1.0, None, ALU.mult, ALU.max, accum_out=top[t // 2][:, t % 2 : t % 2 + 1])
             d_bank.append(bank)
             d_win.append(win)
             if t % 2:
                 pair = slice(t - 1, t + 1)
-                nc.vector.scalar_tensor_tensor(bias[:, pair], top[:, pair], -1.0, tau_t[:, pair], ALU.mult, ALU.mult)
+                nc.vector.scalar_tensor_tensor(bias[:, pair], top[t // 2][:], -1.0, tau_t[:, pair], ALU.mult, ALU.mult)
+        y_diff_last = held([P, 1, H], F32, "y_diff_last", tag="top1")
+        nc.vector.tensor_tensor(y_diff_last[:, 0, :], y_last[:, :H], fetched_last[:], ALU.subtract)
 
         w1_codes = held([P, N], U32, "w1_codes")
         w1_scales = held([P, N], U8, "w1_scales")
@@ -167,20 +172,21 @@ def tile_picked_twtpxbegl_none_p_kernel(tc, x_words, x_scales, wa, wb, tau, gt, 
             z_planes = held([P, PACK, width], BF16, "z_planes%d" % c)
             ea = held([P, PACK, width], F32, "ea%d" % c)
             mixed = held([P, PACK, width], F32, "mixed%d" % c, tag="mixed")
-            group = 2
             for t in range(PACK):
                 nc.scalar.activation(ea[:, t, :], d_win[t][:].indirect(n1_t[:, lo // 16 : hi // 16]), ACT.Exp, bias=bias[:, t : t + 1], scale=tau_t[:, t : t + 1])
-            for first in range(0, PACK, group):
-                ts = slice(first, first + group)
-                nc.vector.tensor_tensor(mixed[:, ts, :], ea[:, ts, :], y_diff[:, ts, lo:hi], ALU.mult)
+            for ts in (slice(0, 2), slice(2, 3), slice(3, 4)):
+                diff = y_diff_last[:, :, lo:hi] if ts.start == PACK - 1 else y_diff[:, ts, lo:hi]
+                nc.vector.tensor_tensor(mixed[:, ts, :], ea[:, ts, :], diff, ALU.mult)
                 for t in range(ts.start, ts.stop):
                     nc.vector.scalar_tensor_tensor(z_planes[:, t, :], d_bank[t][:, lo:hi], gt_neg_half[:, t : t + 1], mixed[:, t, :], ALU.mult, ALU.add)
             z_rows[c] = z_planes
 
-        def weave_z(c, weave):
+        def weave_z(c, split):
             lo, hi = Z_CHUNKS[c]
             z_woven[c] = held([P, hi - lo, PACK], BF16, "z_woven%d" % c)
-            weave(z_woven[c][:], z_rows[c][:])
+            if split:
+                weave_vector(z_woven[c][:, :split, :], z_rows[c][:, :, :split], 8)
+            weave_scalar(z_woven[c][:, split:, :], z_rows[c][:, :, split:], 8)
 
         def quantise_z(c, tag=None):
             lo, hi = Z_CHUNKS[c]
@@ -200,8 +206,8 @@ def tile_picked_twtpxbegl_none_p_kernel(tc, x_words, x_scales, wa, wb, tau, gt, 
         top2 = [held([P, 1], F32, "top2_%d" % b) for b in range(PACK)]
         make_z(0)
         make_z(1)
-        weave_z(0, weave_scalar)
-        weave_z(1, weave_vector)
+        weave_z(0, 0)
+        weave_z(1, 160)
         quantise_z(0, tag="ea1")
         first_rows(0, None, top2_part[:])
         quantise_z(1)
@@ -220,10 +226,12 @@ def tile_picked_twtpxbegl_none_p_kernel(tc, x_words, x_scales, wa, wb, tau, gt, 
                 nc.vector.tensor_scalar(h_win[b][:, :H], bank[:], 1.0, None, ALU.mult, ALU.max, accum_out=top2[b][:])
             nc.vector.scalar_tensor_tensor(bias2[:, b : b + 1], top2[b][:], -1.0, tau2_t[:, b : b + 1], ALU.mult, ALU.mult)
         for b in range(PACK):
-            for c in range(PACK):
-                ea2 = ring.tile([P, H], F32, name="members")
-                nc.scalar.activation(ea2[:], h_win[b][:].indirect(n3_t[:, 32 * c : 32 * (c + 1)]), ACT.Exp, bias=bias2[:, b : b + 1], scale=tau2_t[:, b : b + 1])
-                nc.vector.tensor_reduce(sums[:, b, c * P : (c + 1) * P], ea2[:].rearrange("p (j t) -> p j t", t=PACK), AX.X, ALU.add)
+            parts = 2 if b == PACK - 1 else 1
+            for part in range(parts):
+                count = W // parts
+                ea2 = ring.tile([P, count], F32, name="members")
+                nc.scalar.activation(ea2[:], h_win[b][:].indirect(n3_t[:, part * count // 16 : (part + 1) * count // 16]), ACT.Exp, bias=bias2[:, b : b + 1], scale=tau2_t[:, b : b + 1])
+                nc.vector.tensor_reduce(sums[:, b, part * count // PACK : (part + 1) * count // PACK], ea2[:].rearrange("p (j t) -> p j t", t=PACK), AX.X, ALU.add)
 
         logs = held([P, PACK, H], F32, "logs", tag="h_win%d" % (PACK - 1))
         pieces = [(0, 0, H), (1, 0, H), (2, 0, H), (3, 0, HALF), (3, HALF, H)]

from contextlib import ExitStack

import concourse.mybir as mybir

K, T, S, N, H, W = 512, 2048, 512, 512, 512, 2048
FLOPS = 3 * 2 * 512 * 512 * 512

F32 = mybir.dt.float32
BF16 = mybir.dt.bfloat16
I32 = mybir.dt.int32
U32 = mybir.dt.uint32
U16 = mybir.dt.uint16
U8 = mybir.dt.uint8
FP8X4 = mybir.dt.float8_e4m3fn_x4
ACT = mybir.ActivationFunctionType
ALU = mybir.AluOpType
AX = mybir.AxisListType

P = 128
PACK = 4
HALF = 256
Z_CHUNKS = ((0, 256), (256, 512))


def tile_picked_twtpxbegl_none_p_kernel(tc, x_words, x_scales, wa, wb, tau, gt, w1, tau2, offs, two, n1, n2, n3, out):
    nc = tc.nc
    with ExitStack() as ctx:
        keep = ctx.enter_context(tc.tile_pool(name="keep", bufs=1))
        ring = ctx.enter_context(tc.tile_pool(name="ring", bufs=3))
        stage = ctx.enter_context(tc.tile_pool(name="stage", bufs=1))
        psum = ctx.enter_context(tc.psum_pool(name="psum", bufs=1))

        def held(shape, dtype, name, tag=None):
            return keep.tile(shape, dtype, name=name, tag=tag or name, align_bytes=64)

        def staged(shape, dtype, name, offset):
            return stage.tile(shape, dtype, name=name, align_bytes=64, offset=offset)

        def load_list(src, name):
            tile = keep.tile(list(src.shape), U16, name=name)
            nc.sync.dma_start(tile[:], src)
            return tile

        def load_rows(w, cols, name):
            raw = held([P, PACK, cols.stop - cols.start], F32, name)
            nc.sync.dma_start(out=raw[:], in_=w[:, cols].rearrange("(p j) c -> p j c", j=PACK))
            return raw

        def weave_views(woven, planes, run):
            return (woven.rearrange("p (c i) t -> p c t i", i=run), planes.rearrange("p t (c i) -> p c t i", i=run))

        def weave_vector(woven, planes, run=4):
            dst, src = weave_views(woven, planes, run)
            nc.vector.tensor_copy(out=dst, in_=src)

        def weave_scalar(woven, planes, run=4):
            dst, src = weave_views(woven, planes, run)
            nc.scalar.activation(dst, src, ACT.Copy)

        def quantise(codes, scales, woven):
            nc.vector.quantize_mx(out=codes.bitcast(FP8X4), scales=scales, in_=woven.rearrange("p c t -> p (c t)"))

        def product(acc, lhs, rhs):
            nc.tensor.matmul_mx(out=acc, lhsT=lhs[0].bitcast(FP8X4), lhsT_scale=lhs[1], rhs=rhs[0].bitcast(FP8X4), rhs_scale=rhs[1], start=True, stop=True)

        scale_table = held([P, T], U8, "scale_table")
        nc.gpsimd.memset(scale_table[:].bitcast(I32), 0)
        offs_t = load_list(offs, "offs_t")
        for q in range(4):
            nc.scalar.dma_start(out=scale_table[32 * q : 32 * q + 4, :].bitcast(I32), in_=x_scales[0, 4 * q : 4 * q + 4, :].bitcast(I32))
        halves = [slice(0, HALF), slice(HALF, 2 * HALF)]
        wa_raw = [load_rows(wa, cols, "wa_raw%d" % h) for h, cols in enumerate(halves)]
        two_t = load_list(two, "two_t")
        word_table = held([P, T], U32, "word_table")
        nc.sync.dma_start(out=word_table[:].bitcast(I32), in_=x_words[0].rearrange("p n t -> p (n t)").bitcast(I32))
        gt_t = held([P, PACK], F32, "gt_t")
        nc.sync.dma_start(out=gt_t[:], in_=gt.rearrange("(p t) o -> p (t o)", t=PACK))
        wb_raw = [load_rows(wb, cols, "wb_raw%d" % h) for h, cols in enumerate(halves)]
        n2_t = load_list(n2, "n2_t")
        tau_t = held([P, PACK], F32, "tau_t")
        nc.sync.dma_start(out=tau_t[:], in_=tau.rearrange("(p t) o -> p (t o)", t=PACK))
        n1_t = load_list(n1, "n1_t")
        w1_raw = load_rows(w1, slice(0, N), "w1_raw")
        n3_t = load_list(n3, "n3_t")
        tau2_t = held([P, PACK], F32, "tau2_t")
        with nc.allow_non_contiguous_dma(reason="one rate a partition"):
            nc.sync.dma_start(out=tau2_t[:], in_=tau2.rearrange("(b p) o -> p (b o)", p=P))

        def pick(table, lst, picked):
            nc.vector.tensor_copy(picked[:], table[:].indirect(lst[:]))
            return picked

        def deal(picked, dtype, name, tag=None):
            dealt = held([P, S], dtype, name, tag=tag)
            run = 4 if dtype == U32 else 16
            nc.vector.tensor_copy(out=dealt[:].rearrange("p (t c i) -> p c t i", t=PACK, i=run), in_=picked[:].rearrange("p (c i t) -> p c t i", t=PACK, i=run))
            return dealt


        xy_scales = deal(pick(scale_table, offs_t, held([P, S], U8, "xy_scales_picked")), U8, "xy_scales")
        wa_q = (held([P, H], U32, "wa_codes"), held([P, H], U8, "wa_scales"))
        for h, cols in enumerate(halves):
            woven = held([P, HALF, PACK], BF16, "wa_woven%d" % h, tag=None)
            weave_scalar(woven[:], wa_raw[h][:])
            quantise(wa_q[0][:, cols], wa_q[1][:, cols], woven[:])
        gt_neg_half = held([P, PACK], F32, "gt_neg_half")
        nc.scalar.activation(gt_neg_half[:], gt_t[:], ACT.Copy, scale=-0.5)
        xy = (deal(pick(word_table, offs_t, staged([P, S], U32, "xy_words_picked", 0)), U32, "xy_words"), xy_scales)
        xd_words_picked = pick(word_table, two_t, staged([P, S], U32, "xd_words_picked", 1024))
        xd_scales_picked = pick(scale_table, two_t, staged([P, S], U8, "xd_scales_picked", 0))
        xd = (deal(xd_words_picked, U32, "xd_words"), deal(xd_scales_picked, U8, "xd_scales"))
        wb_q = (held([P, H], U32, "wb_codes"), held([P, H], U8, "wb_scales"))
        for h, cols in enumerate(halves):
            woven = staged([P, HALF, PACK], BF16, "wb_woven1", 1024) if h else held([P, HALF, PACK], BF16, "wb_woven0")
            (weave_vector if h else weave_scalar)(woven[:], wb_raw[h][:])
            quantise(wb_q[0][:, cols], wb_q[1][:, cols], woven[:])

        gt_twice = held([P, PACK], F32, "gt_twice", tag="wb_raw0")
        nc.scalar.activation(gt_twice[:], gt_t[:], ACT.Copy, scale=2.0)
        quarter = held([P, 1], F32, "quarter")
        nc.gpsimd.memset(quarter[:], 0.25)

        def rows(pair, t):
            return (pair[0][:, t * P : (t + 1) * P], pair[1][:, t * P : (t + 1) * P])

        h_win = [held([P, 2 * W], F32, "h_win%d" % t) for t in range(PACK)]
        y_diff = held([P, PACK - 1, H], F32, "y_diff")
        for t in range(PACK):
            bank = psum.tile([P, H], F32, name="y%d" % t, tag="bank%d" % t)
            product(bank[:], rows(xy, t), (wa_q[0][:], wa_q[1][:]))
            win = held([P, H + 16], F32, "y_win%d" % t)
            nc.scalar.activation(win[:, :H], bank[:], ACT.Copy, scale=gt_twice[:, t : t + 1])
            fetched = held([P, H], F32, "y_fetched%d" % t)
            nc.scalar.activation(fetched[:], win[:].indirect(n2_t[:]), ACT.Copy)
            if t < PACK - 1:
                nc.gpsimd.tensor_tensor(y_diff[:, t, :], win[:, :H], fetched[:], ALU.subtract)
        y_last, fetched_last = win, fetched

        d_bank, d_win = [], []
        top = [held([P, 2], F32, "top%d" % pair) for pair in range(2)]
        bias = held([P, PACK], F32, "bias")
        for t in range(PACK):
            bank = psum.tile([P, H], F32, name="d%d" % t, tag="bank%d" % (PACK + t))
            product(bank[:], rows(xd, t), (wb_q[0][:], wb_q[1][:]))
            win = held([P, H], F32, "d_win%d" % t)
            nc.vector.tensor_scalar(win[:], bank[:], 1.0, None, ALU.mult, ALU.max, accum_out=top[t // 2][:, t % 2 : t % 2 + 1])
            d_bank.append(bank)
            d_win.append(win)
            if t % 2:
                pair = slice(t - 1, t + 1)
                nc.vector.scalar_tensor_tensor(bias[:, pair], top[t // 2][:], -1.0, tau_t[:, pair], ALU.mult, ALU.mult)
        y_diff_last = held([P, 1, H], F32, "y_diff_last", tag="top1")
        nc.vector.tensor_tensor(y_diff_last[:, 0, :], y_last[:, :H], fetched_last[:], ALU.subtract)

        w1_codes = held([P, N], U32, "w1_codes")
        w1_scales = held([P, N], U8, "w1_scales")

        def quantise_w1(b):
            cols = slice(b * P, (b + 1) * P)
            woven = held([P, P, PACK], BF16, "w1_woven%d" % b, tag="top2_0") if b else staged([P, P, PACK], BF16, "w1_woven0", 1024)
            weave_vector(woven[:], w1_raw[:, :, cols])
            quantise(w1_codes[:, cols], w1_scales[:, cols], woven[:])

        quantise_w1(0)

        top2_part = held([P, 1], F32, "top2_part")
        z_rows, z_woven, z_q = {}, {}, {}

        def make_z(c):
            lo, hi = Z_CHUNKS[c]
            width = hi - lo
            z_planes = held([P, PACK, width], BF16, "z_planes%d" % c)
            ea = held([P, PACK, width], F32, "ea%d" % c)
            mixed = held([P, PACK, width], F32, "mixed%d" % c, tag="mixed")
            for t in range(PACK):
                nc.scalar.activation(ea[:, t, :], d_win[t][:].indirect(n1_t[:, lo // 16 : hi // 16]), ACT.Exp, bias=bias[:, t : t + 1], scale=tau_t[:, t : t + 1])
            for ts in (slice(0, 2), slice(2, 3), slice(3, 4)):
                diff = y_diff_last[:, :, lo:hi] if ts.start == PACK - 1 else y_diff[:, ts, lo:hi]
                nc.vector.tensor_tensor(mixed[:, ts, :], ea[:, ts, :], diff, ALU.mult)
                for t in range(ts.start, ts.stop):
                    nc.vector.scalar_tensor_tensor(z_planes[:, t, :], d_bank[t][:, lo:hi], gt_neg_half[:, t : t + 1], mixed[:, t, :], ALU.mult, ALU.add)
            z_rows[c] = z_planes

        def weave_z(c, split):
            lo, hi = Z_CHUNKS[c]
            z_woven[c] = held([P, hi - lo, PACK], BF16, "z_woven%d" % c)
            if split:
                weave_vector(z_woven[c][:, :split, :], z_rows[c][:, :, :split], 8)
            weave_scalar(z_woven[c][:, split:, :], z_rows[c][:, :, split:], 8)

        def quantise_z(c, tag=None):
            lo, hi = Z_CHUNKS[c]
            z_q[c] = (held([P, hi - lo], U32, "z_codes%d" % c, tag=tag), held([P, hi - lo], U8, "z_scales%d" % c))
            quantise(z_q[c][0][:], z_q[c][1][:], z_woven[c][:])

        def h_product(bank, b, c):
            lo, hi = Z_CHUNKS[c]
            product(bank[:, lo:hi], rows((w1_codes, w1_scales), b), (z_q[c][0][:], z_q[c][1][:]))

        def first_rows(c, start, top_so_far):
            lo, hi = Z_CHUNKS[c]
            bank = psum.tile([P, H], F32, name="h0_%d" % c, tag="bank%d" % c)
            h_product(bank, 0, c)
            nc.vector.tensor_scalar(h_win[0][:, lo:hi], bank[:, lo:hi], 1.0, start, ALU.mult, ALU.max, accum_out=top_so_far)

        top2 = [held([P, 1], F32, "top2_%d" % b) for b in range(PACK)]
        make_z(0)
        make_z(1)
        weave_z(0, 0)
        weave_z(1, 160)
        quantise_z(0, tag="ea1")
        first_rows(0, None, top2_part[:])
        quantise_z(1)
        first_rows(1, top2_part[:], top2[0][:])

        bias2 = held([P, PACK], F32, "bias2")
        h_rows = [h_win[0]]
        sums = held([P, PACK, H], F32, "sums")
        for b in range(PACK):
            if b:
                quantise_w1(b)
                bank = psum.tile([P, H], F32, name="h%d" % b, tag="bank%d" % b)
                for c in range(len(Z_CHUNKS)):
                    h_product(bank, b, c)
                h_rows.append(bank)
                nc.vector.tensor_scalar(h_win[b][:, :H], bank[:], 1.0, None, ALU.mult, ALU.max, accum_out=top2[b][:])
            nc.vector.scalar_tensor_tensor(bias2[:, b : b + 1], top2[b][:], -1.0, tau2_t[:, b : b + 1], ALU.mult, ALU.mult)
        for b in range(PACK):
            parts = 2 if b == PACK - 1 else 1
            for part in range(parts):
                count = W // parts
                ea2 = ring.tile([P, count], F32, name="members")
                nc.scalar.activation(ea2[:], h_win[b][:].indirect(n3_t[:, part * count // 16 : (part + 1) * count // 16]), ACT.Exp, bias=bias2[:, b : b + 1], scale=tau2_t[:, b : b + 1])
                nc.vector.tensor_reduce(sums[:, b, part * count // PACK : (part + 1) * count // PACK], ea2[:].rearrange("p (j t) -> p j t", t=PACK), AX.X, ALU.add)

        logs = held([P, PACK, H], F32, "logs", tag="h_win%d" % (PACK - 1))
        pieces = [(0, 0, H), (1, 0, H), (2, 0, H), (3, 0, HALF), (3, HALF, H)]
        for b, lo, hi in pieces:
            nc.scalar.activation(logs[:, b, lo:hi], sums[:, b, lo:hi], ACT.Ln, bias=quarter[:])
            result = held([P, hi - lo], F32, "result%d_%d" % (b, lo))
            nc.vector.scalar_tensor_tensor(result[:], h_rows[b][:, lo:hi], -0.5, logs[:, b, lo:hi], ALU.mult, ALU.add)
            nc.sync.dma_start(out=out[b * P : (b + 1) * P, lo:hi], in_=result[:])
